import numpy as np
import ml_dtypes


def mxq(x, axis, fmt="e4m3"):
    dtype, down = {"e4m3": (ml_dtypes.float8_e4m3fn, 7), "e5m2": (ml_dtypes.float8_e5m2, 14)}[fmt]
    v = np.moveaxis(np.asarray(x, np.float32).astype(ml_dtypes.bfloat16).astype(np.float64), axis, -1)
    blocks = v.reshape(v.shape[:-1] + (-1, 32))
    amax = np.abs(blocks).max(-1, keepdims=True)
    byte = np.maximum(np.where(amax > 0, np.frexp(amax)[1] - 1 + 127, 0) - down, 1)
    scale = np.exp2(byte - 127.0)
    codes = (blocks / scale).astype(np.float32).astype(dtype).astype(np.float64)
    return np.moveaxis((codes * scale).reshape(v.shape), -1, axis)


WIDE = False


def mx_kscale(k):
    if not WIDE:
        return np.ones(k)
    levels = np.array([10, -10, 5, -5, 0])
    if k % 512:
        return np.exp2(np.random.permutation(np.resize(levels, k // 32))).repeat(32)
    a = np.empty((k // 512, 16))
    for p in range(k // 512):
        a[p, :8] = np.random.permutation(np.resize(levels, 8))
        for g in range(8):
            far = levels[np.abs(levels - a[p, g]) >= 10]
            a[p, g + 8] = far[np.random.randint(len(far))]
    return np.exp2(a.ravel()).repeat(32)


def f64(x):
    return np.asarray(x).astype(np.float64)


def striped(idx):
    return np.tile(idx.reshape(-1, 16).T, (8, 1)).astype(np.uint16)


def unstriped(offs):
    return offs[:16].T.reshape(-1).astype(np.int64)


def striped8(idx):
    return np.concatenate([x.reshape(-1, 16).T for x in idx]).astype(np.uint16)


def runs(offs, k):
    lists = np.stack([offs[16 * r : 16 * r + 16].T.reshape(-1) for r in range(8)]).astype(np.int64)
    return lists[np.arange(k) % 512 // 64]


def pack_weight(w):
    k, n = w.shape
    w = f64(np.asarray(w, np.float32).astype(ml_dtypes.bfloat16)).reshape(k // 32, 32, n)
    amax = np.abs(w).max(1)
    byte = np.clip(np.where(amax > 0, np.frexp(amax)[1] - 1 + 127 - 7, 1), 1, 254)
    scaled = (w * np.exp2(127.0 - byte)[:, None, :]).reshape(k, n).astype(np.float32)
    words = np.ascontiguousarray(scaled.reshape(k // 512, 128, 4, n).transpose(0, 1, 3, 2)).astype(ml_dtypes.float8_e4m3fn).view(np.uint8)
    return words, np.ascontiguousarray(byte.astype(np.uint8).reshape(k // 512, 16, n))


def unpack_weight(words, scales):
    g, p, n, _ = words.shape
    vals = np.ascontiguousarray(words).view(ml_dtypes.float8_e4m3fn).astype(np.float64) * np.repeat(np.exp2(scales.astype(np.float64) - 127.0), 8, axis=1)[..., None]
    return vals.transpose(0, 1, 3, 2).reshape(g * 512, n)

def planes(y):
    n, m = y.shape
    v = y.astype(np.float32).astype(ml_dtypes.bfloat16).astype(np.float64).reshape(n // 32, 32, m)
    top = np.abs(v).max(1)
    byte = np.clip(np.where(top > 0, np.frexp(top)[1] - 1 + 127 - 7, 1), 1, 254)
    codes = (v * np.exp2(127.0 - byte)[:, None, :]).reshape(n, m).astype(np.float32).astype(ml_dtypes.float8_e4m3fn).view(np.uint8)
    words = codes.reshape(n // 512, 128, 4, m).transpose(0, 1, 3, 2)
    return np.ascontiguousarray(words), np.ascontiguousarray(byte.astype(np.uint8).reshape(n // 512, 16, m))


K, T, S, V, H, C = 512, 2048, 1024, 512, 512, 512


def setup_inputs():
    n = np.random.standard_normal
    s = mx_kscale(K)[:, None]
    packed_xT = pack_weight(n((K, T)) * s)
    packed_w1 = pack_weight(n((K, H)) / np.sqrt(K) / s)
    return {
        "x_words": packed_xT[0],
        "x_scales": packed_xT[1],
        "w1_words": packed_w1[0],
        "w1_scales": packed_w1[1],
        "gs": (np.random.uniform(0.5, 1.5, (K, 1)) / s).astype(np.float32),
        "offs": striped(np.random.permutation(T)[:S]),
        "order": striped8(np.stack([np.random.permutation(S) for _ in range(8)])),
        "cand": striped(np.random.permutation(T)[:C]),
    }


def reference(x_words, x_scales, w1_words, w1_scales, gs, offs, order, cand):
    x_cand = unpack_weight(x_words, x_scales)[:, unstriped(cand)]
    xq = unpack_weight(x_words, x_scales)[:, unstriped(offs)]
    h = unpack_weight(w1_words, w1_scales).T @ xq
    o = h[np.arange(H)[:, None], runs(order, H)]
    mx = o.reshape(H, V, 2).max(axis=2)
    mn = o.reshape(H, V, 2).min(axis=2)
    z = f64(gs) * (mx - (0.5 * mn))
    out_0 = 0.0625 * ((x_cand.T @ mxq(z, 0, "e4m3")))
    return (out_0,) + planes(out_0)

@@ -1,0 +1,170 @@
+from contextlib import ExitStack
+
+import concourse.mybir as mybir
+
+K, T, S, V, H, C = 512, 2048, 1024, 512, 512, 512
+FLOPS = 2 * K * H * S + 2 * K * C * V
+
+F32 = mybir.dt.float32
+BF16 = mybir.dt.bfloat16
+I32 = mybir.dt.int32
+U32 = mybir.dt.uint32
+U16 = mybir.dt.uint16
+U8 = mybir.dt.uint8
+FP8X4 = mybir.dt.float8_e4m3fn_x4
+ALU = mybir.AluOpType
+ACT = mybir.ActivationFunctionType
+
+P = 128
+PACK = 4
+BANK = 512
+UNIT = 128
+CHUNKS = (256, 128, 128)
+
+
+def tile_picked_candwide_none_po_kernel(
+    tc, x_words, x_scales, w1_words, w1_scales, gs, offs, order, cand, out_0, out_1, out_2
+):
+    nc = tc.nc
+    with ExitStack() as ctx:
+        keep = ctx.enter_context(tc.tile_pool(name="keep", bufs=1))
+        psum = ctx.enter_context(tc.psum_pool(name="psum", bufs=1))
+
+        def sb(name, shape, dtype):
+            return keep.tile(shape, dtype, name=name, align_bytes=64)
+
+        offs_t = sb("offs_t", [P, S // 16], U16)
+        order_t = sb("order_t", [P, S // 16], U16)
+        cand_t = sb("cand_t", [P, C // 16], U16)
+        xw = sb("xw", [P, T], U32)
+        xs = sb("xs", [P, T], U8)
+        ww = sb("ww", [P, H], U32)
+        ws = sb("ws", [P, H], U8)
+        g = sb("g", [P, PACK], F32)
+
+        nc.vector.memset(ws[:].bitcast(I32), 0)
+        nc.sync.dma_start(offs_t[:], offs)
+        for q in range(4):
+            rows = x_scales[0, 4 * q : 4 * q + 4, :].bitcast(I32)
+            nc.sync.dma_start(xs[32 * q : 32 * q + 32, :].bitcast(I32), rows.unsqueeze(0).broadcast_to([8, 4, T // 4]))
+        nc.sync.dma_start(xw[:].bitcast(I32), x_words[0].rearrange("p n t -> p (n t)").bitcast(I32))
+        nc.sync.dma_start(cand_t[:], cand)
+        nc.sync.dma_start(ww[:].bitcast(I32), w1_words[0].rearrange("p n t -> p (n t)").bitcast(I32))
+        nc.sync.dma_start(g[:], gs.rearrange("(p t) o -> p (t o)", t=PACK))
+        for q in range(4):
+            nc.sync.dma_start(ws[32 * q : 32 * q + 4, :].bitcast(I32), w1_scales[0, 4 * q : 4 * q + 4, :].bitcast(I32))
+        nc.sync.dma_start(order_t[:], order)
+
+        half_g = sb("half_g", [P, PACK], F32)
+        sign_g = sb("sign_g", [P, PACK], F32)
+        slope = sb("slope", [P, PACK], F32)
+        gain = sb("gain", [P, PACK], F32)
+        nc.scalar.activation(half_g[:], g[:], ACT.Copy, scale=0.5)
+        nc.scalar.activation(sign_g[:], g[:], ACT.Sign)
+        nc.scalar.activation(slope[:], sign_g[:], ACT.Copy, scale=0.75, bias=-1.25)
+        nc.scalar.activation(gain[:], sign_g[:], ACT.Copy, scale=1.5, bias=0.5)
+
+        def deal(dst, src):
+            nc.vector.tensor_copy(
+                dst[:].rearrange("p (t m) -> p m t", t=PACK), src[:].rearrange("p (m t) -> p m t", t=PACK)
+            )
+
+        tok_s = sb("tok_s", [P, S], U8)
+        cand_s = sb("cand_s", [P, C], U8)
+        nc.vector.tensor_copy(tok_s[:], xs[:].indirect(offs_t[:]))
+        nc.vector.tensor_copy(cand_s[:], xs[:].indirect(cand_t[:]))
+        wwd = sb("wwd", [P, H], U32)
+        wsd = sb("wsd", [P, H], U8)
+        deal(wwd, ww)
+        deal(wsd, ws)
+        halves = S // BANK
+        tok_w = [sb("tok_w%d" % u, [P, BANK], U32) for u in range(halves)]
+        h = [sb("h%d" % t, [P, S], F32) for t in range(PACK)]
+        for u in range(halves):
+            cols = slice(u * BANK, (u + 1) * BANK)
+            nc.vector.tensor_copy(tok_w[u][:], xw[:].indirect(offs_t[:, u * BANK // 16 : (u + 1) * BANK // 16]))
+            for t in range(PACK):
+                feat = slice(t * P, (t + 1) * P)
+                acc = psum.tile([P, BANK], F32, name="bank%d" % (u * PACK + t))
+                nc.tensor.matmul_mx(
+                    acc[:], lhsT=wwd[:, feat].bitcast(FP8X4), lhsT_scale=wsd[:, feat],
+                    rhs=tok_w[u][:].bitcast(FP8X4), rhs_scale=tok_s[:, cols], start=True, stop=True,
+                )
+                nc.scalar.activation(h[t][:, cols], acc[:], ACT.Copy, scale=half_g[:, t : t + 1])
+
+        cand_w = sb("cand_w", [P, C], U32)
+        cwd = sb("cwd", [P, C], U32)
+        csd = sb("csd", [P, C], U8)
+        nc.vector.tensor_copy(cand_w[:], xw[:].indirect(cand_t[:]))
+        deal(csd, cand_s)
+        deal(cwd, cand_w)
+
+        out_rows = out_0.rearrange("(p t) v -> p t v", t=PACK)
+        out_words = out_1[0].rearrange("p n t -> p (n t)").bitcast(I32)
+        y_scales = sb("y_scales", [P, V], U8)
+
+        v0 = 0
+        for ci, nv in enumerate(CHUNKS):
+            last = ci == len(CHUNKS) - 1
+            z = sb("z%d" % ci, [P, PACK, nv], BF16)
+            pairs = [sb("pairs%d_%d" % (ci, t), [P, 2 * nv], F32) for t in range(PACK)]
+            diff = [sb("diff%d_%d" % (ci, t), [P, nv], F32) for t in range(PACK)]
+            bent = [sb("bent%d_%d" % (ci, t), [P, nv], F32) for t in range(PACK)]
+
+            def gather(t):
+                nc.vector.tensor_copy(pairs[t][:], h[t][:].indirect(order_t[:, v0 // 8 : (v0 + nv) // 8]))
+
+            def step_diff(t):
+                nc.vector.tensor_tensor(diff[t][:], pairs[t][:, 1::2], pairs[t][:, 0::2], ALU.subtract)
+
+            def step_bend(t):
+                nc.vector.scalar_tensor_tensor(
+                    bent[t][:], diff[t][:], slope[:, t : t + 1], diff[t][:], ALU.mult, ALU.max
+                )
+
+            def step_z(t):
+                nc.vector.scalar_tensor_tensor(
+                    z[:, t, :], bent[t][:], gain[:, t : t + 1], pairs[t][:, 0::2], ALU.mult, ALU.add
+                )
+
+            steps = (gather, step_diff, step_bend, step_z)
+            for wave in range(PACK + len(steps) - 1):
+                for depth, step in enumerate(steps):
+                    if 0 <= wave - depth < PACK:
+                        step(wave - depth)
+
+            for ui in range(nv // UNIT):
+                c0 = v0 + ui * UNIT
+                unit = c0 // UNIT
+                woven = sb("woven%d" % unit, [P, UNIT, PACK], BF16)
+                src = z[:, :, ui * UNIT : (ui + 1) * UNIT].rearrange("p t v -> p v t")
+                if last:
+                    nc.vector.tensor_copy(woven[:], src)
+                else:
+                    nc.scalar.copy(woven[:], src)
+                z_w = sb("z_w%d" % unit, [P, UNIT], U32)
+                z_s = sb("z_s%d" % unit, [P, UNIT], U8)
+                nc.vector.quantize_mx(z_w[:].bitcast(FP8X4), z_s[:], woven[:].rearrange("p v t -> p (v t)"))
+                acc = psum.tile([P, PACK, UNIT], F32, name="bank%d" % unit)
+                for t in range(PACK):
+                    rows = slice(t * P, (t + 1) * P)
+                    nc.tensor.matmul_mx(
+                        acc[:, t, :], lhsT=cwd[:, rows].bitcast(FP8X4), lhsT_scale=csd[:, rows],
+                        rhs=z_w[:].bitcast(FP8X4), rhs_scale=z_s[:], start=True, stop=True,
+                    )
+                y_bf = sb("y_bf%d" % unit, [P, UNIT, PACK], BF16)
+                y = sb("y%d" % unit, [P, PACK, UNIT], F32)
+                nc.scalar.activation(y_bf[:], acc[:].rearrange("p t v -> p v t"), ACT.Copy, scale=0.0625)
+                nc.scalar.activation(y[:], acc[:], ACT.Copy, scale=0.0625)
+                y_w = sb("y_w%d" % unit, [P, UNIT], U32)
+                nc.vector.quantize_mx(
+                    y_w[:].bitcast(FP8X4), y_scales[:, c0 : c0 + UNIT], y_bf[:].rearrange("p v t -> p (v t)")
+                )
+                nc.sync.dma_start(out_rows[:, :, c0 : c0 + UNIT], y[:])
+                nc.sync.dma_start(out_words[:, c0 : c0 + UNIT], y_w[:].bitcast(I32))
+            v0 = v0 + nv
+
+        for q in range(4):
+            nc.scalar.dma_start(
+                out_2[0, 4 * q : 4 * q + 4, :].bitcast(I32), y_scales[32 * q : 32 * q + 4, :].bitcast(I32)
+            )

@@ -19,7 +19,6 @@ P = 128
 PACK = 4
 BANK = 512
 UNIT = 128
-CHUNKS = (256, 128, 128)
 
 
 def tile_picked_candwide_none_po_kernel(
@@ -38,21 +37,24 @@ def tile_picked_candwide_none_po_kernel(
         cand_t = sb("cand_t", [P, C // 16], U16)
         xw = sb("xw", [P, T], U32)
         xs = sb("xs", [P, T], U8)
-        ww = sb("ww", [P, H], U32)
+        ww = sb("undealt", [P, H], U32)
         ws = sb("ws", [P, H], U8)
         g = sb("g", [P, PACK], F32)
 
-        nc.vector.memset(ws[:].bitcast(I32), 0)
+        def load_scales(dst, src):
+            for q in range(4):
+                rows = src[0, 4 * q : 4 * q + 4, :].bitcast(I32)
+                nc.sync.dma_start(
+                    dst[32 * q : 32 * q + 32, :].bitcast(I32), rows.unsqueeze(0).broadcast_to([8, 4, rows.shape[1]])
+                )
+
         nc.sync.dma_start(offs_t[:], offs)
-        for q in range(4):
-            rows = x_scales[0, 4 * q : 4 * q + 4, :].bitcast(I32)
-            nc.sync.dma_start(xs[32 * q : 32 * q + 32, :].bitcast(I32), rows.unsqueeze(0).broadcast_to([8, 4, T // 4]))
+        load_scales(xs, x_scales)
         nc.sync.dma_start(xw[:].bitcast(I32), x_words[0].rearrange("p n t -> p (n t)").bitcast(I32))
         nc.sync.dma_start(cand_t[:], cand)
-        nc.sync.dma_start(ww[:].bitcast(I32), w1_words[0].rearrange("p n t -> p (n t)").bitcast(I32))
         nc.sync.dma_start(g[:], gs.rearrange("(p t) o -> p (t o)", t=PACK))
-        for q in range(4):
-            nc.sync.dma_start(ws[32 * q : 32 * q + 4, :].bitcast(I32), w1_scales[0, 4 * q : 4 * q + 4, :].bitcast(I32))
+        load_scales(ws, w1_scales)
+        nc.sync.dma_start(ww[:].bitcast(I32), w1_words[0].rearrange("p n t -> p (n t)").bitcast(I32))
         nc.sync.dma_start(order_t[:], order)
 
         half_g = sb("half_g", [P, PACK], F32)
@@ -75,24 +77,25 @@ def tile_picked_candwide_none_po_kernel(
         nc.vector.tensor_copy(cand_s[:], xs[:].indirect(cand_t[:]))
         wwd = sb("wwd", [P, H], U32)
         wsd = sb("wsd", [P, H], U8)
-        deal(wwd, ww)
         deal(wsd, ws)
+        deal(wwd, ww)
         halves = S // BANK
         tok_w = [sb("tok_w%d" % u, [P, BANK], U32) for u in range(halves)]
         h = [sb("h%d" % t, [P, S], F32) for t in range(PACK)]
         for u in range(halves):
-            cols = slice(u * BANK, (u + 1) * BANK)
             nc.vector.tensor_copy(tok_w[u][:], xw[:].indirect(offs_t[:, u * BANK // 16 : (u + 1) * BANK // 16]))
-            for t in range(PACK):
-                feat = slice(t * P, (t + 1) * P)
-                acc = psum.tile([P, BANK], F32, name="bank%d" % (u * PACK + t))
+        for t in range(PACK):
+            feat = slice(t * P, (t + 1) * P)
+            for u in range(halves):
+                cols = slice(u * BANK, (u + 1) * BANK)
+                acc = psum.tile([P, BANK], F32, name="bank%d" % (t * halves + u))
                 nc.tensor.matmul_mx(
                     acc[:], lhsT=wwd[:, feat].bitcast(FP8X4), lhsT_scale=wsd[:, feat],
                     rhs=tok_w[u][:].bitcast(FP8X4), rhs_scale=tok_s[:, cols], start=True, stop=True,
                 )
                 nc.scalar.activation(h[t][:, cols], acc[:], ACT.Copy, scale=half_g[:, t : t + 1])
 
-        cand_w = sb("cand_w", [P, C], U32)
+        cand_w = sb("undealt", [P, C], U32)
         cwd = sb("cwd", [P, C], U32)
         csd = sb("csd", [P, C], U8)
         nc.vector.tensor_copy(cand_w[:], xw[:].indirect(cand_t[:]))
@@ -103,66 +106,66 @@ def tile_picked_candwide_none_po_kernel(
         out_words = out_1[0].rearrange("p n t -> p (n t)").bitcast(I32)
         y_scales = sb("y_scales", [P, V], U8)
 
-        v0 = 0
-        for ci, nv in enumerate(CHUNKS):
-            last = ci == len(CHUNKS) - 1
-            z = sb("z%d" % ci, [P, PACK, nv], BF16)
-            pairs = [sb("pairs%d_%d" % (ci, t), [P, 2 * nv], F32) for t in range(PACK)]
-            diff = [sb("diff%d_%d" % (ci, t), [P, nv], F32) for t in range(PACK)]
-            bent = [sb("bent%d_%d" % (ci, t), [P, nv], F32) for t in range(PACK)]
+        units = V // UNIT
 
-            def gather(t):
-                nc.vector.tensor_copy(pairs[t][:], h[t][:].indirect(order_t[:, v0 // 8 : (v0 + nv) // 8]))
+        picked = sb("picked", [P, 2, PACK, 2 * UNIT], F32)
 
-            def step_diff(t):
-                nc.vector.tensor_tensor(diff[t][:], pairs[t][:, 1::2], pairs[t][:, 0::2], ALU.subtract)
+        def gather(unit):
+            entries = order_t[:, unit * UNIT // 8 : (unit + 1) * UNIT // 8]
+            for t in range(PACK):
+                nc.vector.tensor_copy(picked[:, unit % 2, t, :], h[t][:].indirect(entries))
 
-            def step_bend(t):
+        def score(unit):
+            last = unit == units - 1
+            c0 = unit * UNIT
+            first, second = picked[:, unit % 2, :, 0::2], picked[:, unit % 2, :, 1::2]
+            diff = sb("diff", [P, PACK, UNIT], F32)
+            shared = 0 if last else PACK - 1 if unit == 0 else PACK
+            if shared:
+                nc.gpsimd.tensor_tensor(diff[:, :shared, :], second[:, :shared, :], first[:, :shared, :], ALU.subtract)
+            for t in range(shared, PACK):
+                nc.vector.tensor_tensor(diff[:, t, :], second[:, t, :], first[:, t, :], ALU.subtract)
+            for t in range(PACK):
                 nc.vector.scalar_tensor_tensor(
-                    bent[t][:], diff[t][:], slope[:, t : t + 1], diff[t][:], ALU.mult, ALU.max
+                    diff[:, t, :], diff[:, t, :], slope[:, t : t + 1], diff[:, t, :], ALU.mult, ALU.max
                 )
-
-            def step_z(t):
+            z = sb("z%d" % unit, [P, PACK, UNIT], BF16)
+            for t in range(PACK):
                 nc.vector.scalar_tensor_tensor(
-                    z[:, t, :], bent[t][:], gain[:, t : t + 1], pairs[t][:, 0::2], ALU.mult, ALU.add
+                    z[:, t, :], diff[:, t, :], gain[:, t : t + 1], first[:, t, :], ALU.mult, ALU.add
                 )
-
-            steps = (gather, step_diff, step_bend, step_z)
-            for wave in range(PACK + len(steps) - 1):
-                for depth, step in enumerate(steps):
-                    if 0 <= wave - depth < PACK:
-                        step(wave - depth)
-
-            for ui in range(nv // UNIT):
-                c0 = v0 + ui * UNIT
-                unit = c0 // UNIT
-                woven = sb("woven%d" % unit, [P, UNIT, PACK], BF16)
-                src = z[:, :, ui * UNIT : (ui + 1) * UNIT].rearrange("p t v -> p v t")
-                if last:
-                    nc.vector.tensor_copy(woven[:], src)
-                else:
-                    nc.scalar.copy(woven[:], src)
-                z_w = sb("z_w%d" % unit, [P, UNIT], U32)
-                z_s = sb("z_s%d" % unit, [P, UNIT], U8)
-                nc.vector.quantize_mx(z_w[:].bitcast(FP8X4), z_s[:], woven[:].rearrange("p v t -> p (v t)"))
-                acc = psum.tile([P, PACK, UNIT], F32, name="bank%d" % unit)
-                for t in range(PACK):
-                    rows = slice(t * P, (t + 1) * P)
-                    nc.tensor.matmul_mx(
-                        acc[:, t, :], lhsT=cwd[:, rows].bitcast(FP8X4), lhsT_scale=csd[:, rows],
-                        rhs=z_w[:].bitcast(FP8X4), rhs_scale=z_s[:], start=True, stop=True,
-                    )
-                y_bf = sb("y_bf%d" % unit, [P, UNIT, PACK], BF16)
-                y = sb("y%d" % unit, [P, PACK, UNIT], F32)
-                nc.scalar.activation(y_bf[:], acc[:].rearrange("p t v -> p v t"), ACT.Copy, scale=0.0625)
-                nc.scalar.activation(y[:], acc[:], ACT.Copy, scale=0.0625)
-                y_w = sb("y_w%d" % unit, [P, UNIT], U32)
-                nc.vector.quantize_mx(
-                    y_w[:].bitcast(FP8X4), y_scales[:, c0 : c0 + UNIT], y_bf[:].rearrange("p v t -> p (v t)")
+            woven = sb("woven%d" % unit, [P, UNIT, PACK], BF16)
+            if last:
+                nc.vector.tensor_copy(woven[:], z[:].rearrange("p t v -> p v t"))
+            else:
+                nc.scalar.copy(woven[:], z[:].rearrange("p t v -> p v t"))
+            z_w = sb("z_w%d" % unit, [P, UNIT], U32)
+            z_s = sb("z_s%d" % unit, [P, UNIT], U8)
+            nc.vector.quantize_mx(z_w[:].bitcast(FP8X4), z_s[:], woven[:].rearrange("p v t -> p (v t)"))
+            acc = psum.tile([P, PACK, UNIT], F32, name="bank%d" % unit)
+            for t in range(PACK):
+                rows = slice(t * P, (t + 1) * P)
+                nc.tensor.matmul_mx(
+                    acc[:, t, :], lhsT=cwd[:, rows].bitcast(FP8X4), lhsT_scale=csd[:, rows],
+                    rhs=z_w[:].bitcast(FP8X4), rhs_scale=z_s[:], start=True, stop=True,
                 )
-                nc.sync.dma_start(out_rows[:, :, c0 : c0 + UNIT], y[:])
-                nc.sync.dma_start(out_words[:, c0 : c0 + UNIT], y_w[:].bitcast(I32))
-            v0 = v0 + nv
+            y_bf = sb("y_bf%d" % unit, [P, UNIT, PACK], BF16)
+            y = sb("y%d" % unit, [P, PACK, UNIT], F32)
+            nc.scalar.activation(y_bf[:], acc[:].rearrange("p t v -> p v t"), ACT.Copy, scale=0.0625)
+            nc.scalar.activation(y[:], acc[:], ACT.Copy, scale=0.0625)
+            y_w = sb("y_w%d" % unit, [P, UNIT], U32)
+            nc.vector.quantize_mx(
+                y_w[:].bitcast(FP8X4), y_scales[:, c0 : c0 + UNIT], y_bf[:].rearrange("p v t -> p (v t)")
+            )
+            nc.sync.dma_start(out_rows[:, :, c0 : c0 + UNIT], y[:])
+            nc.sync.dma_start(out_words[:, c0 : c0 + UNIT], y_w[:].bitcast(I32))
+
+        gather(0)
+        gather(1)
+        for unit in range(units):
+            score(unit)
+            if unit + 2 < units:
+                gather(unit + 2)
 
         for q in range(4):
             nc.scalar.dma_start(

@@ -37,34 +37,32 @@ def tile_picked_candwide_none_po_kernel(
         cand_t = sb("cand_t", [P, C // 16], U16)
         xw = sb("xw", [P, T], U32)
         xs = sb("xs", [P, T], U8)
-        ww = sb("undealt", [P, H], U32)
+        ww = sb("ww", [P, H], U32)
         ws = sb("ws", [P, H], U8)
         g = sb("g", [P, PACK], F32)
 
-        def load_scales(dst, src):
+        def load_scales(dst, src, queues):
             for q in range(4):
                 rows = src[0, 4 * q : 4 * q + 4, :].bitcast(I32)
-                nc.sync.dma_start(
+                queues[q].dma_start(
                     dst[32 * q : 32 * q + 32, :].bitcast(I32), rows.unsqueeze(0).broadcast_to([8, 4, rows.shape[1]])
                 )
 
         nc.sync.dma_start(offs_t[:], offs)
-        load_scales(xs, x_scales)
+        load_scales(xs, x_scales, (nc.sync,) * 4)
+        nc.sync.dma_start(ww[:].bitcast(I32), w1_words[0].rearrange("p n t -> p (n t)").bitcast(I32))
         nc.sync.dma_start(xw[:].bitcast(I32), x_words[0].rearrange("p n t -> p (n t)").bitcast(I32))
         nc.sync.dma_start(cand_t[:], cand)
+        load_scales(ws, w1_scales, (nc.sync,) * 4)
         nc.sync.dma_start(g[:], gs.rearrange("(p t) o -> p (t o)", t=PACK))
-        load_scales(ws, w1_scales)
-        nc.sync.dma_start(ww[:].bitcast(I32), w1_words[0].rearrange("p n t -> p (n t)").bitcast(I32))
         nc.sync.dma_start(order_t[:], order)
 
-        half_g = sb("half_g", [P, PACK], F32)
+        quarter_g = sb("quarter_g", [P, PACK], F32)
         sign_g = sb("sign_g", [P, PACK], F32)
-        slope = sb("slope", [P, PACK], F32)
         gain = sb("gain", [P, PACK], F32)
-        nc.scalar.activation(half_g[:], g[:], ACT.Copy, scale=0.5)
+        nc.scalar.activation(quarter_g[:], g[:], ACT.Copy, scale=0.25)
         nc.scalar.activation(sign_g[:], g[:], ACT.Sign)
-        nc.scalar.activation(slope[:], sign_g[:], ACT.Copy, scale=0.75, bias=-1.25)
-        nc.scalar.activation(gain[:], sign_g[:], ACT.Copy, scale=1.5, bias=0.5)
+        nc.scalar.activation(gain[:], sign_g[:], ACT.Copy, scale=3.0)
 
         def deal(dst, src):
             nc.vector.tensor_copy(
@@ -77,8 +75,10 @@ def tile_picked_candwide_none_po_kernel(
         nc.vector.tensor_copy(cand_s[:], xs[:].indirect(cand_t[:]))
         wwd = sb("wwd", [P, H], U32)
         wsd = sb("wsd", [P, H], U8)
-        deal(wsd, ws)
-        deal(wwd, ww)
+        for dst, src in ((wwd, ww), (wsd, ws)):
+            nc.gpsimd.tensor_copy(
+                dst[:].rearrange("p (t m) -> p t m", t=PACK), src[:].rearrange("p (m t) -> p t m", t=PACK)
+            )
         halves = S // BANK
         tok_w = [sb("tok_w%d" % u, [P, BANK], U32) for u in range(halves)]
         h = [sb("h%d" % t, [P, S], F32) for t in range(PACK)]
@@ -93,14 +93,14 @@ def tile_picked_candwide_none_po_kernel(
                     acc[:], lhsT=wwd[:, feat].bitcast(FP8X4), lhsT_scale=wsd[:, feat],
                     rhs=tok_w[u][:].bitcast(FP8X4), rhs_scale=tok_s[:, cols], start=True, stop=True,
                 )
-                nc.scalar.activation(h[t][:, cols], acc[:], ACT.Copy, scale=half_g[:, t : t + 1])
+                nc.scalar.activation(h[t][:, cols], acc[:], ACT.Copy, scale=quarter_g[:, t : t + 1])
 
-        cand_w = sb("undealt", [P, C], U32)
+        cand_w = sb("cand_w", [P, C], U32)
         cwd = sb("cwd", [P, C], U32)
-        csd = sb("csd", [P, C], U8)
+        csd = sb("ws", [P, C], U8)
         nc.vector.tensor_copy(cand_w[:], xw[:].indirect(cand_t[:]))
-        deal(csd, cand_s)
         deal(cwd, cand_w)
+        deal(csd, cand_s)
 
         out_rows = out_0.rearrange("(p t) v -> p t v", t=PACK)
         out_words = out_1[0].rearrange("p n t -> p (n t)").bitcast(I32)
@@ -108,31 +108,28 @@ def tile_picked_candwide_none_po_kernel(
 
         units = V // UNIT
 
-        picked = sb("picked", [P, 2, PACK, 2 * UNIT], F32)
-
         def gather(unit):
+            picked = sb("turn%d" % (unit % 3), [P, PACK, 2 * UNIT], F32)
             entries = order_t[:, unit * UNIT // 8 : (unit + 1) * UNIT // 8]
             for t in range(PACK):
-                nc.vector.tensor_copy(picked[:, unit % 2, t, :], h[t][:].indirect(entries))
+                nc.vector.tensor_copy(picked[:, t, :], h[t][:].indirect(entries))
+            return picked
 
-        def score(unit):
+        def score(unit, picked, work):
             last = unit == units - 1
-            c0 = unit * UNIT
-            first, second = picked[:, unit % 2, :, 0::2], picked[:, unit % 2, :, 1::2]
-            diff = sb("diff", [P, PACK, UNIT], F32)
-            shared = 0 if last else PACK - 1 if unit == 0 else PACK
-            if shared:
-                nc.gpsimd.tensor_tensor(diff[:, :shared, :], second[:, :shared, :], first[:, :shared, :], ALU.subtract)
-            for t in range(shared, PACK):
-                nc.vector.tensor_tensor(diff[:, t, :], second[:, t, :], first[:, t, :], ALU.subtract)
-            for t in range(PACK):
-                nc.vector.scalar_tensor_tensor(
-                    diff[:, t, :], diff[:, t, :], slope[:, t : t + 1], diff[:, t, :], ALU.mult, ALU.max
-                )
+            first, second = picked[:, :, 0::2], picked[:, :, 1::2]
+            diff, total = work[:, 0], work[:, 1]
+            size = sb("turn%d" % ((unit + 2) % 3), [P, PACK, UNIT], F32)
+            width = PACK // 2 if unit == 0 else PACK
+            for t0 in range(0, PACK, width):
+                ts = slice(t0, t0 + width)
+                (nc.vector if last else nc.gpsimd).tensor_tensor(diff[:, ts], second[:, ts], first[:, ts], ALU.subtract)
+                nc.scalar.activation(size[:, ts], diff[:, ts], ACT.Abs)
+            (nc.vector if last or unit == 0 else nc.gpsimd).tensor_tensor(total, second, first, ALU.add)
             z = sb("z%d" % unit, [P, PACK, UNIT], BF16)
             for t in range(PACK):
                 nc.vector.scalar_tensor_tensor(
-                    z[:, t, :], diff[:, t, :], gain[:, t : t + 1], first[:, t, :], ALU.mult, ALU.add
+                    z[:, t, :], size[:, t, :], gain[:, t : t + 1], total[:, t, :], ALU.mult, ALU.add
                 )
             woven = sb("woven%d" % unit, [P, UNIT, PACK], BF16)
             if last:
@@ -149,23 +146,45 @@ def tile_picked_candwide_none_po_kernel(
                     acc[:, t, :], lhsT=cwd[:, rows].bitcast(FP8X4), lhsT_scale=csd[:, rows],
                     rhs=z_w[:].bitcast(FP8X4), rhs_scale=z_s[:], start=True, stop=True,
                 )
-            y_bf = sb("y_bf%d" % unit, [P, UNIT, PACK], BF16)
-            y = sb("y%d" % unit, [P, PACK, UNIT], F32)
-            nc.scalar.activation(y_bf[:], acc[:].rearrange("p t v -> p v t"), ACT.Copy, scale=0.0625)
-            nc.scalar.activation(y[:], acc[:], ACT.Copy, scale=0.0625)
-            y_w = sb("y_w%d" % unit, [P, UNIT], U32)
-            nc.vector.quantize_mx(
-                y_w[:].bitcast(FP8X4), y_scales[:, c0 : c0 + UNIT], y_bf[:].rearrange("p v t -> p (v t)")
-            )
-            nc.sync.dma_start(out_rows[:, :, c0 : c0 + UNIT], y[:])
-            nc.sync.dma_start(out_words[:, c0 : c0 + UNIT], y_w[:].bitcast(I32))
+            return acc
 
-        gather(0)
-        gather(1)
+        def round_out(unit, acc, y_bf):
+            nc.scalar.activation(y_bf, acc[:].rearrange("p t v -> p v t"), ACT.Copy, scale=0.0625)
+
+        def store_out(unit, acc, name):
+            y = sb(name, [P, PACK, UNIT], F32)
+            if unit == units - 2:
+                nc.vector.tensor_scalar(y[:], acc[:], 0.0625, None, ALU.mult)
+            else:
+                nc.scalar.activation(y[:], acc[:], ACT.Copy, scale=0.0625)
+            nc.sync.dma_start(out_rows[:, :, unit * UNIT : (unit + 1) * UNIT], y[:])
+
+        def store_planes(c0, width, name):
+            cols = slice(c0, c0 + width)
+            y_w = sb(name, [P, width], U32)
+            nc.vector.quantize_mx(
+                y_w[:].bitcast(FP8X4), y_scales[:, cols], y_bf[:, cols, :].rearrange("p v t -> p (v t)")
+            )
+            nc.sync.dma_start(out_words[:, cols], y_w[:].bitcast(I32))
+
+        y_bf = sb("y_bf", [P, V, PACK], BF16)
+        sums = []
+        picked = [gather(0), gather(1)]
         for unit in range(units):
-            score(unit)
+            if unit < units - 1:
+                work = sb("work", [P, 2, PACK, UNIT], F32)
+            sums.append(score(unit, picked[unit], work))
             if unit + 2 < units:
-                gather(unit + 2)
+                picked.append(gather(unit + 2))
+            round_out(unit, sums[unit], y_bf[:, unit * UNIT : (unit + 1) * UNIT, :])
+            if unit == 0:
+                store_out(0, sums[0], "y0")
+        store_out(1, sums[1], "turn0")
+        store_planes(0, 2 * UNIT, "turn2")
+        store_out(2, sums[2], "y2")
+        store_planes(2 * UNIT, UNIT, "y_w2")
+        store_planes(3 * UNIT, UNIT, "y_w3")
+        store_out(3, sums[3], "y3")
 
         for q in range(4):
             nc.scalar.dma_start(

@@ -50,19 +50,21 @@ def tile_picked_candwide_none_po_kernel(
 
         nc.sync.dma_start(offs_t[:], offs)
         load_scales(xs, x_scales, (nc.sync,) * 4)
+        nc.sync.dma_start(cand_t[:], cand)
         nc.sync.dma_start(ww[:].bitcast(I32), w1_words[0].rearrange("p n t -> p (n t)").bitcast(I32))
         nc.sync.dma_start(xw[:].bitcast(I32), x_words[0].rearrange("p n t -> p (n t)").bitcast(I32))
-        nc.sync.dma_start(cand_t[:], cand)
         load_scales(ws, w1_scales, (nc.sync,) * 4)
         nc.sync.dma_start(g[:], gs.rearrange("(p t) o -> p (t o)", t=PACK))
         nc.sync.dma_start(order_t[:], order)
 
-        quarter_g = sb("quarter_g", [P, PACK], F32)
+        half_g = sb("half_g", [P, PACK], F32)
         sign_g = sb("sign_g", [P, PACK], F32)
+        slope = sb("slope", [P, PACK], F32)
         gain = sb("gain", [P, PACK], F32)
-        nc.scalar.activation(quarter_g[:], g[:], ACT.Copy, scale=0.25)
+        nc.scalar.activation(half_g[:], g[:], ACT.Copy, scale=0.5)
         nc.scalar.activation(sign_g[:], g[:], ACT.Sign)
-        nc.scalar.activation(gain[:], sign_g[:], ACT.Copy, scale=3.0)
+        nc.scalar.activation(slope[:], sign_g[:], ACT.Copy, scale=0.75, bias=-1.25)
+        nc.scalar.activation(gain[:], sign_g[:], ACT.Copy, scale=1.5, bias=0.5)
 
         def deal(dst, src):
             nc.vector.tensor_copy(
@@ -93,7 +95,7 @@ def tile_picked_candwide_none_po_kernel(
                     acc[:], lhsT=wwd[:, feat].bitcast(FP8X4), lhsT_scale=wsd[:, feat],
                     rhs=tok_w[u][:].bitcast(FP8X4), rhs_scale=tok_s[:, cols], start=True, stop=True,
                 )
-                nc.scalar.activation(h[t][:, cols], acc[:], ACT.Copy, scale=quarter_g[:, t : t + 1])
+                nc.scalar.activation(h[t][:, cols], acc[:], ACT.Copy, scale=half_g[:, t : t + 1])
 
         cand_w = sb("cand_w", [P, C], U32)
         cwd = sb("cwd", [P, C], U32)
@@ -108,28 +110,30 @@ def tile_picked_candwide_none_po_kernel(
 
         units = V // UNIT
 
+        picked = sb("picked", [P, 2, PACK, 2 * UNIT], F32)
+
         def gather(unit):
-            picked = sb("turn%d" % (unit % 3), [P, PACK, 2 * UNIT], F32)
             entries = order_t[:, unit * UNIT // 8 : (unit + 1) * UNIT // 8]
             for t in range(PACK):
-                nc.vector.tensor_copy(picked[:, t, :], h[t][:].indirect(entries))
-            return picked
+                nc.vector.tensor_copy(picked[:, unit % 2, t, :], h[t][:].indirect(entries))
 
-        def score(unit, picked, work):
+        def score(unit):
             last = unit == units - 1
-            first, second = picked[:, :, 0::2], picked[:, :, 1::2]
-            diff, total = work[:, 0], work[:, 1]
-            size = sb("turn%d" % ((unit + 2) % 3), [P, PACK, UNIT], F32)
-            width = PACK // 2 if unit == 0 else PACK
-            for t0 in range(0, PACK, width):
-                ts = slice(t0, t0 + width)
-                (nc.vector if last else nc.gpsimd).tensor_tensor(diff[:, ts], second[:, ts], first[:, ts], ALU.subtract)
-                nc.scalar.activation(size[:, ts], diff[:, ts], ACT.Abs)
-            (nc.vector if last or unit == 0 else nc.gpsimd).tensor_tensor(total, second, first, ALU.add)
+            first, second = picked[:, unit % 2, :, 0::2], picked[:, unit % 2, :, 1::2]
+            diff = sb("diff", [P, PACK, UNIT], F32)
+            shared = 0 if last else PACK - 1
+            if shared:
+                nc.gpsimd.tensor_tensor(diff[:, :shared, :], second[:, :shared, :], first[:, :shared, :], ALU.subtract)
+            for t in range(shared, PACK):
+                nc.vector.tensor_tensor(diff[:, t, :], second[:, t, :], first[:, t, :], ALU.subtract)
+            for t in range(PACK):
+                nc.vector.scalar_tensor_tensor(
+                    diff[:, t, :], diff[:, t, :], slope[:, t : t + 1], diff[:, t, :], ALU.mult, ALU.max
+                )
             z = sb("z%d" % unit, [P, PACK, UNIT], BF16)
             for t in range(PACK):
                 nc.vector.scalar_tensor_tensor(
-                    z[:, t, :], size[:, t, :], gain[:, t : t + 1], total[:, t, :], ALU.mult, ALU.add
+                    z[:, t, :], diff[:, t, :], gain[:, t : t + 1], first[:, t, :], ALU.mult, ALU.add
                 )
             woven = sb("woven%d" % unit, [P, UNIT, PACK], BF16)
             if last:
@@ -158,6 +162,7 @@ def tile_picked_candwide_none_po_kernel(
             else:
                 nc.scalar.activation(y[:], acc[:], ACT.Copy, scale=0.0625)
             nc.sync.dma_start(out_rows[:, :, unit * UNIT : (unit + 1) * UNIT], y[:])
+            return y
 
         def store_planes(c0, width, name):
             cols = slice(c0, c0 + width)
@@ -169,22 +174,22 @@ def tile_picked_candwide_none_po_kernel(
 
         y_bf = sb("y_bf", [P, V, PACK], BF16)
         sums = []
-        picked = [gather(0), gather(1)]
+        gather(0)
+        gather(1)
         for unit in range(units):
-            if unit < units - 1:
-                work = sb("work", [P, 2, PACK, UNIT], F32)
-            sums.append(score(unit, picked[unit], work))
+            sums.append(score(unit))
             if unit + 2 < units:
-                picked.append(gather(unit + 2))
-            round_out(unit, sums[unit], y_bf[:, unit * UNIT : (unit + 1) * UNIT, :])
-            if unit == 0:
-                store_out(0, sums[0], "y0")
-        store_out(1, sums[1], "turn0")
-        store_planes(0, 2 * UNIT, "turn2")
+                gather(unit + 2)
+            if unit < units - 1:
+                round_out(unit, sums[unit], y_bf[:, unit * UNIT : (unit + 1) * UNIT, :])
+            if unit < units - 2:
+                store_out(unit, sums[unit], "y%d" % unit)
+        store_planes(0, 2 * UNIT, "diff")
         store_out(2, sums[2], "y2")
         store_planes(2 * UNIT, UNIT, "y_w2")
+        y = store_out(3, sums[3], "y3")
+        nc.vector.tensor_copy(y_bf[:, 3 * UNIT :, :], y[:].rearrange("p t v -> p v t"))
         store_planes(3 * UNIT, UNIT, "y_w3")
-        store_out(3, sums[3], "y3")
 
         for q in range(4):
             nc.scalar.dma_start(

from contextlib import ExitStack

import concourse.mybir as mybir

K, T, S, V, H, C = 512, 2048, 1024, 512, 512, 512
FLOPS = 2 * K * H * S + 2 * K * C * V

F32 = mybir.dt.float32
BF16 = mybir.dt.bfloat16
I32 = mybir.dt.int32
U32 = mybir.dt.uint32
U16 = mybir.dt.uint16
U8 = mybir.dt.uint8
FP8X4 = mybir.dt.float8_e4m3fn_x4
ALU = mybir.AluOpType
ACT = mybir.ActivationFunctionType

P = 128
PACK = 4
BANK = 512
UNIT = 128


def tile_picked_candwide_none_po_kernel(
    tc, x_words, x_scales, w1_words, w1_scales, gs, offs, order, cand, out_0, out_1, out_2
):
    nc = tc.nc
    with ExitStack() as ctx:
        keep = ctx.enter_context(tc.tile_pool(name="keep", bufs=1))
        psum = ctx.enter_context(tc.psum_pool(name="psum", bufs=1))

        def sb(name, shape, dtype):
            return keep.tile(shape, dtype, name=name, align_bytes=64)

        offs_t = sb("offs_t", [P, S // 16], U16)
        order_t = sb("order_t", [P, S // 16], U16)
        cand_t = sb("cand_t", [P, C // 16], U16)
        xw = sb("xw", [P, T], U32)
        xs = sb("xs", [P, T], U8)
        ww = sb("ww", [P, H], U32)
        ws = sb("ws", [P, H], U8)
        g = sb("g", [P, PACK], F32)

        def load_scales(dst, src, queues):
            for q in range(4):
                rows = src[0, 4 * q : 4 * q + 4, :].bitcast(I32)
                queues[q].dma_start(
                    dst[32 * q : 32 * q + 32, :].bitcast(I32), rows.unsqueeze(0).broadcast_to([8, 4, rows.shape[1]])
                )

        nc.sync.dma_start(offs_t[:], offs)
        load_scales(xs, x_scales, (nc.sync,) * 4)
        nc.sync.dma_start(cand_t[:], cand)
        nc.sync.dma_start(ww[:].bitcast(I32), w1_words[0].rearrange("p n t -> p (n t)").bitcast(I32))
        nc.sync.dma_start(xw[:].bitcast(I32), x_words[0].rearrange("p n t -> p (n t)").bitcast(I32))
        load_scales(ws, w1_scales, (nc.sync,) * 4)
        nc.sync.dma_start(g[:], gs.rearrange("(p t) o -> p (t o)", t=PACK))
        nc.sync.dma_start(order_t[:], order)

        half_g = sb("half_g", [P, PACK], F32)
        sign_g = sb("sign_g", [P, PACK], F32)
        slope = sb("slope", [P, PACK], F32)
        gain = sb("gain", [P, PACK], F32)
        nc.scalar.activation(half_g[:], g[:], ACT.Copy, scale=0.5)
        nc.scalar.activation(sign_g[:], g[:], ACT.Sign)
        nc.scalar.activation(slope[:], sign_g[:], ACT.Copy, scale=0.75, bias=-1.25)
        nc.scalar.activation(gain[:], sign_g[:], ACT.Copy, scale=1.5, bias=0.5)

        def deal(dst, src):
            nc.vector.tensor_copy(
                dst[:].rearrange("p (t m) -> p m t", t=PACK), src[:].rearrange("p (m t) -> p m t", t=PACK)
            )

        tok_s = sb("tok_s", [P, S], U8)
        cand_s = sb("cand_s", [P, C], U8)
        nc.vector.tensor_copy(tok_s[:], xs[:].indirect(offs_t[:]))
        nc.vector.tensor_copy(cand_s[:], xs[:].indirect(cand_t[:]))
        wwd = sb("wwd", [P, H], U32)
        wsd = sb("wsd", [P, H], U8)
        for dst, src in ((wwd, ww), (wsd, ws)):
            nc.gpsimd.tensor_copy(
                dst[:].rearrange("p (t m) -> p t m", t=PACK), src[:].rearrange("p (m t) -> p t m", t=PACK)
            )
        halves = S // BANK
        tok_w = [sb("tok_w%d" % u, [P, BANK], U32) for u in range(halves)]
        h = [sb("h%d" % t, [P, S], F32) for t in range(PACK)]
        for u in range(halves):
            nc.vector.tensor_copy(tok_w[u][:], xw[:].indirect(offs_t[:, u * BANK // 16 : (u + 1) * BANK // 16]))
        for t in range(PACK):
            feat = slice(t * P, (t + 1) * P)
            for u in range(halves):
                cols = slice(u * BANK, (u + 1) * BANK)
                acc = psum.tile([P, BANK], F32, name="bank%d" % (t * halves + u))
                nc.tensor.matmul_mx(
                    acc[:], lhsT=wwd[:, feat].bitcast(FP8X4), lhsT_scale=wsd[:, feat],
                    rhs=tok_w[u][:].bitcast(FP8X4), rhs_scale=tok_s[:, cols], start=True, stop=True,
                )
                nc.scalar.activation(h[t][:, cols], acc[:], ACT.Copy, scale=half_g[:, t : t + 1])

        cand_w = sb("cand_w", [P, C], U32)
        cwd = sb("cwd", [P, C], U32)
        csd = sb("ws", [P, C], U8)
        nc.vector.tensor_copy(cand_w[:], xw[:].indirect(cand_t[:]))
        deal(cwd, cand_w)
        deal(csd, cand_s)

        out_rows = out_0.rearrange("(p t) v -> p t v", t=PACK)
        out_words = out_1[0].rearrange("p n t -> p (n t)").bitcast(I32)
        y_scales = sb("y_scales", [P, V], U8)

        units = V // UNIT

        picked = sb("picked", [P, 2, PACK, 2 * UNIT], F32)

        def gather(unit):
            entries = order_t[:, unit * UNIT // 8 : (unit + 1) * UNIT // 8]
            for t in range(PACK):
                nc.vector.tensor_copy(picked[:, unit % 2, t, :], h[t][:].indirect(entries))

        def score(unit):
            last = unit == units - 1
            first, second = picked[:, unit % 2, :, 0::2], picked[:, unit % 2, :, 1::2]
            diff = sb("diff", [P, PACK, UNIT], F32)
            shared = 0 if last else PACK - 1
            if shared:
                nc.gpsimd.tensor_tensor(diff[:, :shared, :], second[:, :shared, :], first[:, :shared, :], ALU.subtract)
            for t in range(shared, PACK):
                nc.vector.tensor_tensor(diff[:, t, :], second[:, t, :], first[:, t, :], ALU.subtract)
            for t in range(PACK):
                nc.vector.scalar_tensor_tensor(
                    diff[:, t, :], diff[:, t, :], slope[:, t : t + 1], diff[:, t, :], ALU.mult, ALU.max
                )
            z = sb("z%d" % unit, [P, PACK, UNIT], BF16)
            for t in range(PACK):
                nc.vector.scalar_tensor_tensor(
                    z[:, t, :], diff[:, t, :], gain[:, t : t + 1], first[:, t, :], ALU.mult, ALU.add
                )
            woven = sb("woven%d" % unit, [P, UNIT, PACK], BF16)
            if last:
                nc.vector.tensor_copy(woven[:], z[:].rearrange("p t v -> p v t"))
            else:
                nc.scalar.copy(woven[:], z[:].rearrange("p t v -> p v t"))
            z_w = sb("z_w%d" % unit, [P, UNIT], U32)
            z_s = sb("z_s%d" % unit, [P, UNIT], U8)
            nc.vector.quantize_mx(z_w[:].bitcast(FP8X4), z_s[:], woven[:].rearrange("p v t -> p (v t)"))
            acc = psum.tile([P, PACK, UNIT], F32, name="bank%d" % unit)
            for t in range(PACK):
                rows = slice(t * P, (t + 1) * P)
                nc.tensor.matmul_mx(
                    acc[:, t, :], lhsT=cwd[:, rows].bitcast(FP8X4), lhsT_scale=csd[:, rows],
                    rhs=z_w[:].bitcast(FP8X4), rhs_scale=z_s[:], start=True, stop=True,
                )
            return acc

        def round_out(unit, acc, y_bf):
            nc.scalar.activation(y_bf, acc[:].rearrange("p t v -> p v t"), ACT.Copy, scale=0.0625)

        def store_out(unit, acc, name):
            y = sb(name, [P, PACK, UNIT], F32)
            if unit == units - 2:
                nc.vector.tensor_scalar(y[:], acc[:], 0.0625, None, ALU.mult)
            else:
                nc.scalar.activation(y[:], acc[:], ACT.Copy, scale=0.0625)
            nc.sync.dma_start(out_rows[:, :, unit * UNIT : (unit + 1) * UNIT], y[:])
            return y

        def store_planes(c0, width, name):
            cols = slice(c0, c0 + width)
            y_w = sb(name, [P, width], U32)
            nc.vector.quantize_mx(
                y_w[:].bitcast(FP8X4), y_scales[:, cols], y_bf[:, cols, :].rearrange("p v t -> p (v t)")
            )
            nc.sync.dma_start(out_words[:, cols], y_w[:].bitcast(I32))

        y_bf = sb("y_bf", [P, V, PACK], BF16)
        sums = []
        gather(0)
        gather(1)
        for unit in range(units):
            sums.append(score(unit))
            if unit + 2 < units:
                gather(unit + 2)
            if unit < units - 1:
                round_out(unit, sums[unit], y_bf[:, unit * UNIT : (unit + 1) * UNIT, :])
            if unit < units - 2:
                store_out(unit, sums[unit], "y%d" % unit)
        store_planes(0, 2 * UNIT, "diff")
        store_out(2, sums[2], "y2")
        store_planes(2 * UNIT, UNIT, "y_w2")
        y = store_out(3, sums[3], "y3")
        nc.vector.tensor_copy(y_bf[:, 3 * UNIT :, :], y[:].rearrange("p t v -> p v t"))
        store_planes(3 * UNIT, UNIT, "y_w3")

        for q in range(4):
            nc.scalar.dma_start(
                out_2[0, 4 * q : 4 * q + 4, :].bitcast(I32), y_scales[32 * q : 32 * q + 4, :].bitcast(I32)
            )
